import numpy as np
import ml_dtypes


def mxq(x, axis, fmt="e4m3"):
    dtype, down = {"e4m3": (ml_dtypes.float8_e4m3fn, 7), "e5m2": (ml_dtypes.float8_e5m2, 14)}[fmt]
    v = np.moveaxis(np.asarray(x, np.float32).astype(ml_dtypes.bfloat16).astype(np.float64), axis, -1)
    blocks = v.reshape(v.shape[:-1] + (-1, 32))
    amax = np.abs(blocks).max(-1, keepdims=True)
    byte = np.maximum(np.where(amax > 0, np.frexp(amax)[1] - 1 + 127, 0) - down, 1)
    scale = np.exp2(byte - 127.0)
    codes = (blocks / scale).astype(np.float32).astype(dtype).astype(np.float64)
    return np.moveaxis((codes * scale).reshape(v.shape), -1, axis)


WIDE = False


def mx_kscale(k):
    if not WIDE:
        return np.ones(k)
    levels = np.array([10, -10, 5, -5, 0])
    if k % 512:
        return np.exp2(np.random.permutation(np.resize(levels, k // 32))).repeat(32)
    a = np.empty((k // 512, 16))
    for p in range(k // 512):
        a[p, :8] = np.random.permutation(np.resize(levels, 8))
        for g in range(8):
            far = levels[np.abs(levels - a[p, g]) >= 10]
            a[p, g + 8] = far[np.random.randint(len(far))]
    return np.exp2(a.ravel()).repeat(32)


def f64(x):
    return np.asarray(x).astype(np.float64)


def striped(idx):
    return np.tile(idx.reshape(-1, 16).T, (8, 1)).astype(np.uint16)


def unstriped(offs):
    return offs[:16].T.reshape(-1).astype(np.int64)


E2M1 = np.array([0.0, 0.5, 1.0, 1.5, 2.0, 3.0, 4.0, 6.0, -0.0, -0.5, -1.0, -1.5, -2.0, -3.0, -4.0, -6.0])


def pack_fp4(w):
    k, n = w.shape
    w = f64(np.asarray(w, np.float32).astype(ml_dtypes.bfloat16)).reshape(k // 32, 32, n)
    amax = np.abs(w).max(1)
    mant, ex = np.frexp(amax / 6.0)
    byte = np.clip(np.where(amax > 0, np.where(mant > 0.5, ex, ex - 1) + 127, 1), 1, 254)
    scaled = (w * np.exp2(127.0 - byte)[:, None, :]).reshape(k, n).astype(np.float32)
    c = np.ascontiguousarray(scaled.reshape(k // 512, 128, 4, n).transpose(0, 1, 3, 2)).astype(ml_dtypes.float4_e2m1fn).view(np.uint8) & 0xF
    words = (c[..., 0::2] | (c[..., 1::2] << 4)).reshape(k // 512, 128, 2 * n)
    return np.ascontiguousarray(words), np.ascontiguousarray(byte.astype(np.uint8).reshape(k // 512, 16, n))


def unpack_fp4(words, scales):
    g, _, n = scales.shape
    words = np.ascontiguousarray(words).reshape(g, 128, n, 2)
    nib = np.empty((g, 128, n, 4), np.uint8)
    nib[..., 0::2] = words & 0xF
    nib[..., 1::2] = words >> 4
    vals = E2M1[nib] * np.repeat(np.exp2(scales.astype(np.float64) - 127.0), 8, axis=1)[..., None]
    return vals.transpose(0, 1, 3, 2).reshape(g * 512, n)


def planes(y):
    n, m = y.shape
    v = y.astype(np.float32).astype(ml_dtypes.bfloat16).astype(np.float64).reshape(n // 32, 32, m)
    top = np.abs(v).max(1)
    byte = np.clip(np.where(top > 0, np.frexp(top)[1] - 1 + 127 - 7, 1), 1, 254)
    codes = (v * np.exp2(127.0 - byte)[:, None, :]).reshape(n, m).astype(np.float32).astype(ml_dtypes.float8_e4m3fn).view(np.uint8)
    words = codes.reshape(n // 512, 128, 4, m).transpose(0, 1, 3, 2)
    return np.ascontiguousarray(words), np.ascontiguousarray(byte.astype(np.uint8).reshape(n // 512, 16, m))


K, T, D, N = 512, 512, 4, 512
P = 2 ** 7


def setup_inputs():
    n = np.random.standard_normal
    s = mx_kscale(K)[:, None]
    packed_xT = pack_fp4(n((K, T)) * s)
    return {
        "x_words": packed_xT[0],
        "x_scales": packed_xT[1],
        "w1": (n((K, N)) / np.sqrt(K) / s).astype(np.float32),
        "gate": (np.tile(np.random.uniform(0.2, 1.0, (D, 1, T)) / np.sqrt(D), (1, P, 1))).astype(np.float32),
        "pos1": striped(np.random.permutation(T)),
        "pos2": striped(np.random.permutation(T)),
        "pos3": striped(np.random.permutation(T)),
        "pos4": striped(np.random.permutation(T)),
    }


def reference(x_words, x_scales, w1, gate, pos1, pos2, pos3, pos4):
    xq = unpack_fp4(x_words, x_scales)
    y = mxq(f64(w1), 0, "e4m3").T @ xq
    out_0 = y + (y[:, unstriped(pos1)] - y) * f64(gate)[0, :1] + (y[:, unstriped(pos2)] - y) * f64(gate)[1, :1] + (y[:, unstriped(pos3)] - y) * f64(gate)[2, :1] + (y[:, unstriped(pos4)] - y) * f64(gate)[3, :1]
    return (out_0,) + planes(out_0)

@@ -1,0 +1,254 @@
+from contextlib import ExitStack
+
+import concourse.mybir as mybir
+from concourse.masks import make_identity
+
+K, T, D, N = 512, 512, 4, 512
+FLOPS = 2 * K * N * T
+
+F32 = mybir.dt.float32
+BF16 = mybir.dt.bfloat16
+I32 = mybir.dt.int32
+U32 = mybir.dt.uint32
+U16 = mybir.dt.uint16
+U8 = mybir.dt.uint8
+FP8X4 = mybir.dt.float8_e4m3fn_x4
+FP4X4 = mybir.dt.float4_e2m1fn_x4
+COPY = mybir.ActivationFunctionType.Copy
+MULT = mybir.AluOpType.mult
+
+P = 128
+PACK = 4
+BLOCKS = N // P
+VB = T // P
+SPARE = 8
+
+
+def tile_picked_wgrand_none_lo_kernel(
+    tc, x_words, x_scales, w1, gate, pos1, pos2, pos3, pos4, out_0, out_1, out_2
+):
+    nc = tc.nc
+    with ExitStack() as ctx:
+        keep = ctx.enter_context(tc.tile_pool(name="keep", bufs=1))
+        ring = ctx.enter_context(tc.tile_pool(name="ring", bufs=6))
+        ps_a = ctx.enter_context(tc.psum_pool(name="ps_a", bufs=2))
+        ps_f = ctx.enter_context(tc.psum_pool(name="ps_f", bufs=2))
+        ps_o = ctx.enter_context(tc.psum_pool(name="ps_o", bufs=1))
+
+        lists = [keep.tile([P, T // 16], U16, name=f"list{d}") for d in range(D)]
+        gates = [keep.tile([P, T], F32, name=f"gate{d}", align_bytes=64) for d in range(D)]
+        w_raw = [keep.tile([P, PACK, P], F32, name=f"w_raw{b}") for b in range(BLOCKS)]
+        xw = keep.tile([P, 2 * T], U8, name="xw", align_bytes=64)
+        xs = keep.tile([P, T], U8, name="xs", align_bytes=64)
+        gate_rows = keep.tile([P, P], F32, name="gate_rows")
+        ident = keep.tile([P, P], F32, name="ident")
+        y = [keep.tile([P, T + SPARE], F32, name=f"y{b}") for b in range(BLOCKS)]
+
+        w_view = w1.rearrange("(p j) c -> p j c", j=PACK)
+        pos = [pos1, pos2, pos3, pos4]
+
+        def load_w(b):
+            nc.sync.dma_start(out=w_raw[b][:], in_=w_view[:, :, b * P : (b + 1) * P])
+
+        def load_edge(d):
+            nc.sync.dma_start(lists[d][:], pos[d])
+            nc.sync.dma_start(out=gates[d][:], in_=gate[d])
+
+        nc.vector.memset(xs[:].bitcast(I32), 0)
+        load_w(0)
+        for q in range(4):
+            nc.sync.dma_start(
+                out=xs[32 * q : 32 * q + 4, :].bitcast(I32),
+                in_=x_scales[0, 4 * q : 4 * q + 4, :].bitcast(I32),
+            )
+        nc.sync.dma_start(out=xw[:].bitcast(I32), in_=x_words[0].bitcast(I32))
+        load_edge(0)
+        load_edge(1)
+        load_edge(2)
+        load_w(1)
+        load_edge(3)
+        load_w(2)
+        load_w(3)
+        make_identity(nc, ident[:])
+        nc.gpsimd.memset(gate_rows[:], 0.0)
+        for d in range(D):
+            nc.sync.dma_start(
+                out=gate_rows[VB * d : VB * (d + 1), :],
+                in_=gate[d, 0, :].rearrange("(vb v) -> vb v", v=P),
+            )
+        for b in range(BLOCKS):
+            nc.gpsimd.memset(y[b][:, T:], 0.0)
+
+        def project(b):
+            grouped = keep.tile([P, PACK * P], BF16, name=f"w_bf{b}", align_bytes=64)
+            dst = grouped[:].rearrange("p (c i j) -> p c j i", i=4, j=PACK)
+            src = w_raw[b][:].rearrange("p j (c i) -> p c j i", i=4)
+            if b == 0:
+                nc.vector.tensor_copy(out=dst[:, :16], in_=src[:, :16])
+                nc.scalar.activation(dst[:, 16:], src[:, 16:], COPY)
+            else:
+                nc.scalar.activation(dst, src, COPY)
+            codes = keep.tile([P, P], U32, name=f"w_codes{b}", align_bytes=64)
+            scales = keep.tile([P, P], U8, name=f"w_scales{b}", align_bytes=64)
+            nc.vector.quantize_mx(out=codes[:].bitcast(FP8X4), scales=scales[:], in_=grouped[:])
+            width = T // 2 if b == 0 else T
+            for c0 in range(0, T, width):
+                acc = ps_a.tile([P, T], F32, name="acc", tag="bank")
+                nc.tensor.matmul_mx(
+                    out=acc[:, :width],
+                    lhsT=codes[:].bitcast(FP8X4),
+                    lhsT_scale=scales[:],
+                    rhs=xw[:, 2 * c0 : 2 * (c0 + width)].bitcast(FP4X4),
+                    rhs_scale=xs[:, c0 : c0 + width],
+                    start=True,
+                    stop=True,
+                )
+                if c0 > 0:
+                    nc.vector.tensor_copy(out=y[b][:, c0 : c0 + width], in_=acc[:, :width])
+                else:
+                    nc.scalar.activation(y[b][:, c0 : c0 + width], acc[:, :width], COPY)
+
+        def turn(out, in_, start, stop):
+            nc.tensor.matmul(out, lhsT=in_, rhs=ident[:], is_transpose=True, start=start, stop=stop)
+
+        own = keep.tile([P, VB, PACK, P], F32, name="own")
+        moved = [keep.tile([P, PACK, P], F32, name=f"moved{vb}") for vb in range(VB)]
+        stay = keep.tile([P, VB], F32, name="stay")
+        junk = keep.tile([P, VB, D], F32, name="terms")
+
+        def make_stay():
+            turned = ps_a.tile([P, T], F32, name="turned", tag="bank")
+            turn(turned[:, :P], gate_rows[:], True, True)
+            by_vb = turned[:, : D * VB].rearrange("p (d vb) -> p vb d", vb=VB)
+            for vb in range(VB):
+                nc.scalar.activation(
+                    junk[:, vb, :], by_vb[:, vb, :], COPY, bias=1.0 / D, scale=-1.0,
+                    accum_out=stay[:, vb : vb + 1],
+                )
+
+        def own_term(b):
+            yt = ps_a.tile([P, VB, P], F32, name="yt", tag="bank")
+            for vb in range(VB):
+                turn(yt[:, vb, :], y[b][:, vb * P : (vb + 1) * P], True, True)
+            for vb in range(VB):
+                nc.scalar.activation(
+                    own[:, vb, :, 32 * b : 32 * (b + 1)],
+                    yt[:, vb, :].rearrange("p (m t) -> p t m", t=PACK),
+                    COPY,
+                    scale=stay[:, vb : vb + 1],
+                )
+
+        def neighbours(b, vb0, vb1, last=False):
+            n = vb1 - vb0
+            total = ps_f.tile([P, VB, P], F32, name="total", tag="total")
+            for d in range(D):
+                z = ring.tile([P, T], F32, name="z", tag="z")
+                nc.vector.tensor_tensor(
+                    z[:, : n * P],
+                    y[b][:].indirect(lists[d][:, vb0 * 8 : vb1 * 8]),
+                    gates[d][:, vb0 * P : vb1 * P],
+                    MULT,
+                )
+                for i in range(n):
+                    turn(
+                        total[:, i, :],
+                        z[:, i * P : (i + 1) * P],
+                        d == 0 and i == 0,
+                        d == D - 1 and i == n - 1,
+                    )
+            for i in range(n):
+                dst = moved[vb0 + i][:, :, 32 * b : 32 * (b + 1)]
+                src = total[:, i, :].rearrange("p (m t) -> p t m", t=PACK)
+                if last:
+                    nc.vector.tensor_copy(out=dst, in_=src)
+                else:
+                    nc.scalar.activation(dst, src, COPY)
+
+        out_rows = out_0.rearrange("(p t) v -> p t v", t=PACK)
+        out_words = out_1[0].rearrange("p c r -> p (c r)")
+        result = {}
+
+        def open_result(vb):
+            bank = ps_o.tile([P, PACK, P], F32, name=f"result{vb}")
+            if vb < VB - 1:
+                result[vb] = [(bank, 0, PACK)]
+            else:
+                second = ps_a.tile([P, PACK, P], F32, name="second", tag="bank")
+                result[vb] = [(bank, 0, 2), (second, 2, PACK)]
+            for tile, t0, t1 in result[vb]:
+                for t in range(t0, t1):
+                    turn(tile[:, t, :], own[:, vb, t, :], t == t0, False)
+
+        def close_result(vb):
+            for tile, t0, t1 in result[vb]:
+                for t in range(t0, t1):
+                    turn(tile[:, t, :], moved[vb][:, t, :], False, t == t1 - 1)
+
+        def finish(vb0, vb1):
+            n = vb1 - vb0
+            staged = keep.tile([P, PACK, n * P], F32, name=f"staged{vb0}")
+            rounded = keep.tile([P, n * P, PACK], BF16, name=f"rounded{vb0}", align_bytes=64)
+            for i in range(n):
+                close_result(vb0 + i)
+                bank = result[vb0 + i][0][0]
+                nc.scalar.activation(staged[:, :, i * P : (i + 1) * P], bank[:], COPY)
+                nc.scalar.activation(
+                    rounded[:, i * P : (i + 1) * P, :], bank[:].rearrange("p t v -> p v t"), COPY
+                )
+            nc.sync.dma_start(out=out_rows[:, :, vb0 * P : vb1 * P], in_=staged[:])
+            return rounded
+
+        def finish_last(vb):
+            staged = keep.tile([P, PACK, P], F32, name="staged_last")
+            rounded = keep.tile([P, P, PACK], BF16, name="rounded_last", align_bytes=64)
+            close_result(vb)
+            (first, a0, a1), (second, b0, b1) = result[vb]
+            nc.scalar.activation(staged[:, a0:a1, :], first[:, a0:a1, :], COPY)
+            nc.vector.tensor_copy(out=staged[:, b0:b1, :], in_=second[:, b0:b1, :])
+            nc.scalar.dma_start(out=out_rows[:, :, vb * P : (vb + 1) * P], in_=staged[:])
+            nc.vector.tensor_copy(
+                out=rounded[:].rearrange("p (c i) t -> p c t i", i=4),
+                in_=staged[:].rearrange("p t (c i) -> p c t i", i=4),
+            )
+            return rounded
+
+        def planes(vb0, vb1, rounded, out_scales):
+            codes = keep.tile([P, (vb1 - vb0) * P], U32, name=f"out_codes{vb0}", align_bytes=64)
+            nc.vector.quantize_mx(
+                out=codes[:].bitcast(FP8X4),
+                scales=out_scales[:, vb0 * P : vb1 * P],
+                in_=rounded[:].rearrange("p v t -> p (v t)"),
+            )
+            nc.sync.dma_start(
+                out=out_words[:, PACK * vb0 * P : PACK * vb1 * P].bitcast(I32),
+                in_=codes[:].bitcast(I32),
+            )
+
+        project(0)
+        project(1)
+        neighbours(0, 0, VB)
+        project(2)
+        project(3)
+        make_stay()
+        for b in range(BLOCKS):
+            own_term(b)
+        neighbours(1, 0, VB)
+        for vb in range(VB):
+            open_result(vb)
+        neighbours(2, 0, 2)
+        neighbours(3, 0, 2)
+        neighbours(2, 2, 4)
+        first = finish(0, 2)
+        neighbours(3, 2, 3)
+        second = finish(2, 3)
+        neighbours(3, 3, 4, last=True)
+        out_scales = keep.tile([P, T], U8, name="out_scales", tag="gate3", align_bytes=64)
+        planes(0, 2, first, out_scales)
+        planes(2, 3, second, out_scales)
+        planes(3, 4, finish_last(3), out_scales)
+        for q in range(4):
+            queue = nc.scalar if q % 2 else nc.sync
+            queue.dma_start(
+                out=out_2[0, 4 * q : 4 * q + 4, :].bitcast(I32),
+                in_=out_scales[32 * q : 32 * q + 4, :].bitcast(I32),
+            )

@@ -30,10 +30,8 @@ def tile_picked_wgrand_none_lo_kernel(
     nc = tc.nc
     with ExitStack() as ctx:
         keep = ctx.enter_context(tc.tile_pool(name="keep", bufs=1))
-        ring = ctx.enter_context(tc.tile_pool(name="ring", bufs=6))
-        ps_a = ctx.enter_context(tc.psum_pool(name="ps_a", bufs=2))
-        ps_f = ctx.enter_context(tc.psum_pool(name="ps_f", bufs=2))
-        ps_o = ctx.enter_context(tc.psum_pool(name="ps_o", bufs=1))
+        ring = ctx.enter_context(tc.tile_pool(name="ring", bufs=D))
+        psum = ctx.enter_context(tc.psum_pool(name="psum", bufs=1))
 
         lists = [keep.tile([P, T // 16], U16, name=f"list{d}") for d in range(D)]
         gates = [keep.tile([P, T], F32, name=f"gate{d}", align_bytes=64) for d in range(D)]
@@ -63,37 +61,39 @@ def tile_picked_wgrand_none_lo_kernel(
             )
         nc.sync.dma_start(out=xw[:].bitcast(I32), in_=x_words[0].bitcast(I32))
         load_edge(0)
-        load_edge(1)
-        load_edge(2)
         load_w(1)
-        load_edge(3)
+        load_edge(1)
+        nc.gpsimd.memset(gate_rows[:], 0.0)
+        nc.sync.dma_start(
+            out=gate_rows[: D * VB, :], in_=gate[:, 0, :].rearrange("d (vb v) -> d vb v", v=P)
+        )
+        load_edge(2)
         load_w(2)
+        load_edge(3)
         load_w(3)
         make_identity(nc, ident[:])
-        nc.gpsimd.memset(gate_rows[:], 0.0)
-        for d in range(D):
-            nc.sync.dma_start(
-                out=gate_rows[VB * d : VB * (d + 1), :],
-                in_=gate[d, 0, :].rearrange("(vb v) -> vb v", v=P),
-            )
         for b in range(BLOCKS):
             nc.gpsimd.memset(y[b][:, T:], 0.0)
 
-        def project(b):
-            grouped = keep.tile([P, PACK * P], BF16, name=f"w_bf{b}", align_bytes=64)
-            dst = grouped[:].rearrange("p (c i j) -> p c j i", i=4, j=PACK)
+        w_bf = {}
+
+        def round_w(b, tag):
+            w_bf[b] = keep.tile([P, PACK * P], BF16, name="w_bf", tag=tag, align_bytes=64)
+            dst = w_bf[b][:].rearrange("p (c i j) -> p c j i", i=4, j=PACK)
             src = w_raw[b][:].rearrange("p j (c i) -> p c j i", i=4)
             if b == 0:
                 nc.vector.tensor_copy(out=dst[:, :16], in_=src[:, :16])
                 nc.scalar.activation(dst[:, 16:], src[:, 16:], COPY)
             else:
                 nc.scalar.activation(dst, src, COPY)
+
+        def project(b, banks):
             codes = keep.tile([P, P], U32, name=f"w_codes{b}", align_bytes=64)
             scales = keep.tile([P, P], U8, name=f"w_scales{b}", align_bytes=64)
-            nc.vector.quantize_mx(out=codes[:].bitcast(FP8X4), scales=scales[:], in_=grouped[:])
+            nc.vector.quantize_mx(out=codes[:].bitcast(FP8X4), scales=scales[:], in_=w_bf[b][:])
             width = T // 2 if b == 0 else T
             for c0 in range(0, T, width):
-                acc = ps_a.tile([P, T], F32, name="acc", tag="bank")
+                acc = psum.tile([P, T], F32, name="acc", tag=banks[c0 // width])
                 nc.tensor.matmul_mx(
                     out=acc[:, :width],
                     lhsT=codes[:].bitcast(FP8X4),
@@ -111,13 +111,13 @@ def tile_picked_wgrand_none_lo_kernel(
         def turn(out, in_, start, stop):
             nc.tensor.matmul(out, lhsT=in_, rhs=ident[:], is_transpose=True, start=start, stop=stop)
 
-        own = keep.tile([P, VB, PACK, P], F32, name="own")
-        moved = [keep.tile([P, PACK, P], F32, name=f"moved{vb}") for vb in range(VB)]
+        own = [keep.tile([P, PACK, P], F32, name=f"own{vb}") for vb in range(VB)]
+        moved = [keep.tile([P, PACK, P], F32, name=f"moved{vb}", align_bytes=64) for vb in range(VB)]
         stay = keep.tile([P, VB], F32, name="stay")
         junk = keep.tile([P, VB, D], F32, name="terms")
 
-        def make_stay():
-            turned = ps_a.tile([P, T], F32, name="turned", tag="bank")
+        def make_stay(bank):
+            turned = psum.tile([P, T], F32, name="turned", tag=bank)
             turn(turned[:, :P], gate_rows[:], True, True)
             by_vb = turned[:, : D * VB].rearrange("p (d vb) -> p vb d", vb=VB)
             for vb in range(VB):
@@ -126,23 +126,29 @@ def tile_picked_wgrand_none_lo_kernel(
                     accum_out=stay[:, vb : vb + 1],
                 )
 
-        def own_term(b):
-            yt = ps_a.tile([P, VB, P], F32, name="yt", tag="bank")
+        def turn_y(b, bank):
+            yt = psum.tile([P, VB, P], F32, name="yt", tag=bank)
             for vb in range(VB):
                 turn(yt[:, vb, :], y[b][:, vb * P : (vb + 1) * P], True, True)
+            return yt
+
+        def own_term(b, yt):
             for vb in range(VB):
                 nc.scalar.activation(
-                    own[:, vb, :, 32 * b : 32 * (b + 1)],
+                    own[vb][:, :, 32 * b : 32 * (b + 1)],
                     yt[:, vb, :].rearrange("p (m t) -> p t m", t=PACK),
                     COPY,
                     scale=stay[:, vb : vb + 1],
                 )
 
-        def neighbours(b, vb0, vb1, last=False):
+        def neighbours(b, vb0, vb1, bank, between, last=False):
             n = vb1 - vb0
-            total = ps_f.tile([P, VB, P], F32, name="total", tag="total")
+            total = psum.tile([P, VB, P], F32, name="total", tag=bank)
             for d in range(D):
-                z = ring.tile([P, T], F32, name="z", tag="z")
+                if b == 0:
+                    z = keep.tile([P, n * P], F32, name="z", tag=f"z0_0_{d}", align_bytes=64)
+                else:
+                    z = ring.tile([P, n * P], F32, name="z", tag="z")
                 nc.vector.tensor_tensor(
                     z[:, : n * P],
                     y[b][:].indirect(lists[d][:, vb0 * 8 : vb1 * 8]),
@@ -156,6 +162,8 @@ def tile_picked_wgrand_none_lo_kernel(
                         d == 0 and i == 0,
                         d == D - 1 and i == n - 1,
                     )
+                for work in between.get(d, ()):
+                    work()
             for i in range(n):
                 dst = moved[vb0 + i][:, :, 32 * b : 32 * (b + 1)]
                 src = total[:, i, :].rearrange("p (m t) -> p t m", t=PACK)
@@ -169,34 +177,28 @@ def tile_picked_wgrand_none_lo_kernel(
         result = {}
 
         def open_result(vb):
-            bank = ps_o.tile([P, PACK, P], F32, name=f"result{vb}")
+            bank = psum.tile([P, PACK, P], F32, name=f"result{vb}")
             if vb < VB - 1:
                 result[vb] = [(bank, 0, PACK)]
             else:
-                second = ps_a.tile([P, PACK, P], F32, name="second", tag="bank")
+                second = psum.tile([P, PACK, P], F32, name="second", tag="B2")
                 result[vb] = [(bank, 0, 2), (second, 2, PACK)]
             for tile, t0, t1 in result[vb]:
                 for t in range(t0, t1):
-                    turn(tile[:, t, :], own[:, vb, t, :], t == t0, False)
+                    turn(tile[:, t, :], own[vb][:, t, :], t == t0, False)
 
         def close_result(vb):
             for tile, t0, t1 in result[vb]:
                 for t in range(t0, t1):
                     turn(tile[:, t, :], moved[vb][:, t, :], False, t == t1 - 1)
 
-        def finish(vb0, vb1):
-            n = vb1 - vb0
-            staged = keep.tile([P, PACK, n * P], F32, name=f"staged{vb0}")
-            rounded = keep.tile([P, n * P, PACK], BF16, name=f"rounded{vb0}", align_bytes=64)
-            for i in range(n):
-                close_result(vb0 + i)
-                bank = result[vb0 + i][0][0]
-                nc.scalar.activation(staged[:, :, i * P : (i + 1) * P], bank[:], COPY)
-                nc.scalar.activation(
-                    rounded[:, i * P : (i + 1) * P, :], bank[:].rearrange("p t v -> p v t"), COPY
-                )
-            nc.sync.dma_start(out=out_rows[:, :, vb0 * P : vb1 * P], in_=staged[:])
-            return rounded
+        def finish(vb, staged, rounded, i):
+            close_result(vb)
+            bank = result[vb][0][0]
+            nc.scalar.activation(staged[:, :, i * P : (i + 1) * P], bank[:], COPY)
+            nc.scalar.activation(
+                rounded[:, i * P : (i + 1) * P, :], bank[:].rearrange("p t v -> p v t"), COPY
+            )
 
         def finish_last(vb):
             staged = keep.tile([P, PACK, P], F32, name="staged_last")
@@ -212,8 +214,8 @@ def tile_picked_wgrand_none_lo_kernel(
             )
             return rounded
 
-        def planes(vb0, vb1, rounded, out_scales):
-            codes = keep.tile([P, (vb1 - vb0) * P], U32, name=f"out_codes{vb0}", align_bytes=64)
+        def planes(vb0, vb1, rounded, out_scales, tag):
+            codes = keep.tile([P, (vb1 - vb0) * P], U32, name="out_codes", tag=tag, align_bytes=64)
             nc.vector.quantize_mx(
                 out=codes[:].bitcast(FP8X4),
                 scales=out_scales[:, vb0 * P : vb1 * P],
@@ -224,28 +226,41 @@ def tile_picked_wgrand_none_lo_kernel(
                 in_=codes[:].bitcast(I32),
             )
 
-        project(0)
-        project(1)
-        neighbours(0, 0, VB)
-        project(2)
-        project(3)
-        make_stay()
-        for b in range(BLOCKS):
-            own_term(b)
-        neighbours(1, 0, VB)
-        for vb in range(VB):
-            open_result(vb)
-        neighbours(2, 0, 2)
-        neighbours(3, 0, 2)
-        neighbours(2, 2, 4)
-        first = finish(0, 2)
-        neighbours(3, 2, 3)
-        second = finish(2, 3)
-        neighbours(3, 3, 4, last=True)
+        staged_a = keep.tile([P, PACK, 2 * P], F32, name="staged_a")
+        first = keep.tile([P, 2 * P, PACK], BF16, name="rounded_a", align_bytes=64)
+        staged_b = keep.tile([P, PACK, P], F32, name="staged_b")
+        second = keep.tile([P, P, PACK], BF16, name="rounded_b", align_bytes=64)
+
+        round_w(0, "w_bf0")
+        project(0, ["B0", "B1"])
+        round_w(1, "w_codes0")
+        make_stay("B0")
+        own_term(0, turn_y(0, "result0"))
+        neighbours(0, 0, VB, "B1", {
+            0: [lambda: project(1, ["B3"]), lambda: round_w(2, "z0_0_0")],
+            1: [lambda: own_term(1, turn_y(1, "result1")), lambda: round_w(3, "z0_0_1")],
+            2: [lambda: project(2, ["B2"])],
+            3: [lambda: project(3, ["B0"]), lambda: own_term(2, turn_y(2, "result2"))],
+        })
+        neighbours(1, 0, 2, "B3", {1: [lambda: own_term(3, turn_y(3, "result3"))]})
+        neighbours(2, 0, 2, "B1", {2: [lambda: open_result(0)]})
+        neighbours(3, 0, 2, "B3", {0: [lambda: open_result(1)], 2: [lambda: open_result(2)]})
+        neighbours(1, 2, 4, "B0", {
+            0: [lambda: finish(0, staged_a, first, 0)],
+            1: [lambda: finish(1, staged_a, first, 1)],
+            3: [lambda: open_result(3)],
+        })
+        nc.sync.dma_start(out=out_rows[:, :, : 2 * P], in_=staged_a[:])
+        neighbours(2, 2, 3, "B1", {})
+        neighbours(3, 2, 3, "B3", {})
+        neighbours(2, 3, 4, "B0", {1: [lambda: finish(2, staged_b, second, 0)]})
+        nc.sync.dma_start(out=out_rows[:, :, 2 * P : 3 * P], in_=staged_b[:])
+        neighbours(3, 3, 4, "B1", {}, last=True)
         out_scales = keep.tile([P, T], U8, name="out_scales", tag="gate3", align_bytes=64)
-        planes(0, 2, first, out_scales)
-        planes(2, 3, second, out_scales)
-        planes(3, 4, finish_last(3), out_scales)
+        planes(0, 2, first, out_scales, "codes_first")
+        third = finish_last(3)
+        planes(2, 3, second, out_scales, "moved3")
+        planes(3, 4, third, out_scales, "codes_last")
         for q in range(4):
             queue = nc.scalar if q % 2 else nc.sync
             queue.dma_start(

from contextlib import ExitStack

import concourse.mybir as mybir
from concourse.masks import make_identity

K, T, D, N = 512, 512, 4, 512
FLOPS = 2 * K * N * T

F32 = mybir.dt.float32
BF16 = mybir.dt.bfloat16
I32 = mybir.dt.int32
U32 = mybir.dt.uint32
U16 = mybir.dt.uint16
U8 = mybir.dt.uint8
FP8X4 = mybir.dt.float8_e4m3fn_x4
FP4X4 = mybir.dt.float4_e2m1fn_x4
COPY = mybir.ActivationFunctionType.Copy
MULT = mybir.AluOpType.mult

P = 128
PACK = 4
BLOCKS = N // P
VB = T // P
SPARE = 8


def tile_picked_wgrand_none_lo_kernel(
    tc, x_words, x_scales, w1, gate, pos1, pos2, pos3, pos4, out_0, out_1, out_2
):
    nc = tc.nc
    with ExitStack() as ctx:
        keep = ctx.enter_context(tc.tile_pool(name="keep", bufs=1))
        ring = ctx.enter_context(tc.tile_pool(name="ring", bufs=D))
        psum = ctx.enter_context(tc.psum_pool(name="psum", bufs=1))

        lists = [keep.tile([P, T // 16], U16, name=f"list{d}") for d in range(D)]
        gates = [keep.tile([P, T], F32, name=f"gate{d}", align_bytes=64) for d in range(D)]
        w_raw = [keep.tile([P, PACK, P], F32, name=f"w_raw{b}") for b in range(BLOCKS)]
        xw = keep.tile([P, 2 * T], U8, name="xw", align_bytes=64)
        xs = keep.tile([P, T], U8, name="xs", align_bytes=64)
        gate_rows = keep.tile([P, P], F32, name="gate_rows")
        ident = keep.tile([P, P], F32, name="ident")
        y = [keep.tile([P, T + SPARE], F32, name=f"y{b}") for b in range(BLOCKS)]

        w_view = w1.rearrange("(p j) c -> p j c", j=PACK)
        pos = [pos1, pos2, pos3, pos4]

        def load_w(b):
            nc.sync.dma_start(out=w_raw[b][:], in_=w_view[:, :, b * P : (b + 1) * P])

        def load_edge(d):
            nc.sync.dma_start(lists[d][:], pos[d])
            nc.sync.dma_start(out=gates[d][:], in_=gate[d])

        nc.vector.memset(xs[:].bitcast(I32), 0)
        load_w(0)
        for q in range(4):
            nc.sync.dma_start(
                out=xs[32 * q : 32 * q + 4, :].bitcast(I32),
                in_=x_scales[0, 4 * q : 4 * q + 4, :].bitcast(I32),
            )
        nc.sync.dma_start(out=xw[:].bitcast(I32), in_=x_words[0].bitcast(I32))
        load_edge(0)
        load_w(1)
        load_edge(1)
        nc.gpsimd.memset(gate_rows[:], 0.0)
        nc.sync.dma_start(
            out=gate_rows[: D * VB, :], in_=gate[:, 0, :].rearrange("d (vb v) -> d vb v", v=P)
        )
        load_edge(2)
        load_w(2)
        load_edge(3)
        load_w(3)
        make_identity(nc, ident[:])
        for b in range(BLOCKS):
            nc.gpsimd.memset(y[b][:, T:], 0.0)

        w_bf = {}

        def round_w(b, tag):
            w_bf[b] = keep.tile([P, PACK * P], BF16, name="w_bf", tag=tag, align_bytes=64)
            dst = w_bf[b][:].rearrange("p (c i j) -> p c j i", i=4, j=PACK)
            src = w_raw[b][:].rearrange("p j (c i) -> p c j i", i=4)
            if b == 0:
                nc.vector.tensor_copy(out=dst[:, :16], in_=src[:, :16])
                nc.scalar.activation(dst[:, 16:], src[:, 16:], COPY)
            else:
                nc.scalar.activation(dst, src, COPY)

        def project(b, banks):
            codes = keep.tile([P, P], U32, name=f"w_codes{b}", align_bytes=64)
            scales = keep.tile([P, P], U8, name=f"w_scales{b}", align_bytes=64)
            nc.vector.quantize_mx(out=codes[:].bitcast(FP8X4), scales=scales[:], in_=w_bf[b][:])
            width = T // 2 if b == 0 else T
            for c0 in range(0, T, width):
                acc = psum.tile([P, T], F32, name="acc", tag=banks[c0 // width])
                nc.tensor.matmul_mx(
                    out=acc[:, :width],
                    lhsT=codes[:].bitcast(FP8X4),
                    lhsT_scale=scales[:],
                    rhs=xw[:, 2 * c0 : 2 * (c0 + width)].bitcast(FP4X4),
                    rhs_scale=xs[:, c0 : c0 + width],
                    start=True,
                    stop=True,
                )
                if c0 > 0:
                    nc.vector.tensor_copy(out=y[b][:, c0 : c0 + width], in_=acc[:, :width])
                else:
                    nc.scalar.activation(y[b][:, c0 : c0 + width], acc[:, :width], COPY)

        def turn(out, in_, start, stop):
            nc.tensor.matmul(out, lhsT=in_, rhs=ident[:], is_transpose=True, start=start, stop=stop)

        own = [keep.tile([P, PACK, P], F32, name=f"own{vb}") for vb in range(VB)]
        moved = [keep.tile([P, PACK, P], F32, name=f"moved{vb}", align_bytes=64) for vb in range(VB)]
        stay = keep.tile([P, VB], F32, name="stay")
        junk = keep.tile([P, VB, D], F32, name="terms")

        def make_stay(bank):
            turned = psum.tile([P, T], F32, name="turned", tag=bank)
            turn(turned[:, :P], gate_rows[:], True, True)
            by_vb = turned[:, : D * VB].rearrange("p (d vb) -> p vb d", vb=VB)
            for vb in range(VB):
                nc.scalar.activation(
                    junk[:, vb, :], by_vb[:, vb, :], COPY, bias=1.0 / D, scale=-1.0,
                    accum_out=stay[:, vb : vb + 1],
                )

        def turn_y(b, bank):
            yt = psum.tile([P, VB, P], F32, name="yt", tag=bank)
            for vb in range(VB):
                turn(yt[:, vb, :], y[b][:, vb * P : (vb + 1) * P], True, True)
            return yt

        def own_term(b, yt):
            for vb in range(VB):
                nc.scalar.activation(
                    own[vb][:, :, 32 * b : 32 * (b + 1)],
                    yt[:, vb, :].rearrange("p (m t) -> p t m", t=PACK),
                    COPY,
                    scale=stay[:, vb : vb + 1],
                )

        def neighbours(b, vb0, vb1, bank, between, last=False):
            n = vb1 - vb0
            total = psum.tile([P, VB, P], F32, name="total", tag=bank)
            for d in range(D):
                if b == 0:
                    z = keep.tile([P, n * P], F32, name="z", tag=f"z0_0_{d}", align_bytes=64)
                else:
                    z = ring.tile([P, n * P], F32, name="z", tag="z")
                nc.vector.tensor_tensor(
                    z[:, : n * P],
                    y[b][:].indirect(lists[d][:, vb0 * 8 : vb1 * 8]),
                    gates[d][:, vb0 * P : vb1 * P],
                    MULT,
                )
                for i in range(n):
                    turn(
                        total[:, i, :],
                        z[:, i * P : (i + 1) * P],
                        d == 0 and i == 0,
                        d == D - 1 and i == n - 1,
                    )
                for work in between.get(d, ()):
                    work()
            for i in range(n):
                dst = moved[vb0 + i][:, :, 32 * b : 32 * (b + 1)]
                src = total[:, i, :].rearrange("p (m t) -> p t m", t=PACK)
                if last:
                    nc.vector.tensor_copy(out=dst, in_=src)
                else:
                    nc.scalar.activation(dst, src, COPY)

        out_rows = out_0.rearrange("(p t) v -> p t v", t=PACK)
        out_words = out_1[0].rearrange("p c r -> p (c r)")
        result = {}

        def open_result(vb):
            bank = psum.tile([P, PACK, P], F32, name=f"result{vb}")
            if vb < VB - 1:
                result[vb] = [(bank, 0, PACK)]
            else:
                second = psum.tile([P, PACK, P], F32, name="second", tag="B2")
                result[vb] = [(bank, 0, 2), (second, 2, PACK)]
            for tile, t0, t1 in result[vb]:
                for t in range(t0, t1):
                    turn(tile[:, t, :], own[vb][:, t, :], t == t0, False)

        def close_result(vb):
            for tile, t0, t1 in result[vb]:
                for t in range(t0, t1):
                    turn(tile[:, t, :], moved[vb][:, t, :], False, t == t1 - 1)

        def finish(vb, staged, rounded, i):
            close_result(vb)
            bank = result[vb][0][0]
            nc.scalar.activation(staged[:, :, i * P : (i + 1) * P], bank[:], COPY)
            nc.scalar.activation(
                rounded[:, i * P : (i + 1) * P, :], bank[:].rearrange("p t v -> p v t"), COPY
            )

        def finish_last(vb):
            staged = keep.tile([P, PACK, P], F32, name="staged_last")
            rounded = keep.tile([P, P, PACK], BF16, name="rounded_last", align_bytes=64)
            close_result(vb)
            (first, a0, a1), (second, b0, b1) = result[vb]
            nc.scalar.activation(staged[:, a0:a1, :], first[:, a0:a1, :], COPY)
            nc.vector.tensor_copy(out=staged[:, b0:b1, :], in_=second[:, b0:b1, :])
            nc.scalar.dma_start(out=out_rows[:, :, vb * P : (vb + 1) * P], in_=staged[:])
            nc.vector.tensor_copy(
                out=rounded[:].rearrange("p (c i) t -> p c t i", i=4),
                in_=staged[:].rearrange("p t (c i) -> p c t i", i=4),
            )
            return rounded

        def planes(vb0, vb1, rounded, out_scales, tag):
            codes = keep.tile([P, (vb1 - vb0) * P], U32, name="out_codes", tag=tag, align_bytes=64)
            nc.vector.quantize_mx(
                out=codes[:].bitcast(FP8X4),
                scales=out_scales[:, vb0 * P : vb1 * P],
                in_=rounded[:].rearrange("p v t -> p (v t)"),
            )
            nc.sync.dma_start(
                out=out_words[:, PACK * vb0 * P : PACK * vb1 * P].bitcast(I32),
                in_=codes[:].bitcast(I32),
            )

        staged_a = keep.tile([P, PACK, 2 * P], F32, name="staged_a")
        first = keep.tile([P, 2 * P, PACK], BF16, name="rounded_a", align_bytes=64)
        staged_b = keep.tile([P, PACK, P], F32, name="staged_b")
        second = keep.tile([P, P, PACK], BF16, name="rounded_b", align_bytes=64)

        round_w(0, "w_bf0")
        project(0, ["B0", "B1"])
        round_w(1, "w_codes0")
        make_stay("B0")
        own_term(0, turn_y(0, "result0"))
        neighbours(0, 0, VB, "B1", {
            0: [lambda: project(1, ["B3"]), lambda: round_w(2, "z0_0_0")],
            1: [lambda: own_term(1, turn_y(1, "result1")), lambda: round_w(3, "z0_0_1")],
            2: [lambda: project(2, ["B2"])],
            3: [lambda: project(3, ["B0"]), lambda: own_term(2, turn_y(2, "result2"))],
        })
        neighbours(1, 0, 2, "B3", {1: [lambda: own_term(3, turn_y(3, "result3"))]})
        neighbours(2, 0, 2, "B1", {2: [lambda: open_result(0)]})
        neighbours(3, 0, 2, "B3", {0: [lambda: open_result(1)], 2: [lambda: open_result(2)]})
        neighbours(1, 2, 4, "B0", {
            0: [lambda: finish(0, staged_a, first, 0)],
            1: [lambda: finish(1, staged_a, first, 1)],
            3: [lambda: open_result(3)],
        })
        nc.sync.dma_start(out=out_rows[:, :, : 2 * P], in_=staged_a[:])
        neighbours(2, 2, 3, "B1", {})
        neighbours(3, 2, 3, "B3", {})
        neighbours(2, 3, 4, "B0", {1: [lambda: finish(2, staged_b, second, 0)]})
        nc.sync.dma_start(out=out_rows[:, :, 2 * P : 3 * P], in_=staged_b[:])
        neighbours(3, 3, 4, "B1", {}, last=True)
        out_scales = keep.tile([P, T], U8, name="out_scales", tag="gate3", align_bytes=64)
        planes(0, 2, first, out_scales, "codes_first")
        third = finish_last(3)
        planes(2, 3, second, out_scales, "moved3")
        planes(3, 4, third, out_scales, "codes_last")
        for q in range(4):
            queue = nc.scalar if q % 2 else nc.sync
            queue.dma_start(
                out=out_2[0, 4 * q : 4 * q + 4, :].bitcast(I32),
                in_=out_scales[32 * q : 32 * q + 4, :].bitcast(I32),
            )
